import numpy as np
import ml_dtypes


def mxq(x, axis, fmt="e4m3"):
    dtype, down = {"e4m3": (ml_dtypes.float8_e4m3fn, 7), "e5m2": (ml_dtypes.float8_e5m2, 14)}[fmt]
    v = np.moveaxis(np.asarray(x, np.float32).astype(ml_dtypes.bfloat16).astype(np.float64), axis, -1)
    blocks = v.reshape(v.shape[:-1] + (-1, 32))
    amax = np.abs(blocks).max(-1, keepdims=True)
    byte = np.maximum(np.where(amax > 0, np.frexp(amax)[1] - 1 + 127, 0) - down, 1)
    scale = np.exp2(byte - 127.0)
    codes = (blocks / scale).astype(np.float32).astype(dtype).astype(np.float64)
    return np.moveaxis((codes * scale).reshape(v.shape), -1, axis)


WIDE = False


def mx_kscale(k):
    if not WIDE:
        return np.ones(k)
    levels = np.array([18, -18])
    if k % 512:
        return np.exp2(np.random.permutation(np.resize(levels, k // 32))).repeat(32)
    a = np.empty((k // 512, 16))
    for p in range(k // 512):
        a[p, :8] = np.random.permutation(np.resize(levels, 8))
        for g in range(8):
            far = levels[np.abs(levels - a[p, g]) >= 10]
            a[p, g + 8] = far[np.random.randint(len(far))]
    return np.exp2(a.ravel()).repeat(32)


def f64(x):
    return np.asarray(x).astype(np.float64)


def striped(idx):
    return np.tile(np.asarray(idx).reshape(-1, 16).T, (8, 1)).astype(np.uint16)


def unstriped(offs):
    return offs[:16].T.reshape(-1).astype(np.int64)

def planes(y):
    n, m = y.shape
    v = y.astype(np.float32).astype(ml_dtypes.bfloat16).astype(np.float64).reshape(n // 32, 32, m)
    top = np.abs(v).max(1)
    byte = np.clip(np.where(top > 0, np.frexp(top)[1] - 1 + 127 - 7, 1), 1, 254)
    codes = (v * np.exp2(127.0 - byte)[:, None, :]).reshape(n, m).astype(np.float32).astype(ml_dtypes.float8_e4m3fn).view(np.uint8)
    words = codes.reshape(n // 512, 128, 4, m).transpose(0, 1, 3, 2)
    return np.ascontiguousarray(words), np.ascontiguousarray(byte.astype(np.uint8).reshape(n // 512, 16, m))


def sig(x):
    return 1.0 / (1.0 + np.exp(-x))


def setup_inputs():
    n = np.random.standard_normal
    uni = np.random.uniform
    idx = np.random.permutation(1024)[:512]
    f_d = mx_kscale(512)
    f_f = mx_kscale(512)
    return {
        "xT": ((0.2 + n((512, 1024))) * f_d[:, None]).astype(np.float32),
        "dyT": (n((512, 1024)) / f_d[:, None]).astype(np.float32),
        "aT": (n((512, 1024))).astype(np.float32),
        "w1": (n((512, 512)) / np.sqrt(512) * f_f[:, None]).astype(np.float32),
        "w2": (n((512, 512)) / np.sqrt(512) * f_d[:, None]).astype(np.float32),
        "gt": np.tile(uni(0.75, 1.3, 1024), (128, 1)).astype(np.float32),
        "gam": np.tile(uni(0.75, 1.3, 512), (128, 1)).astype(np.float32),
        "cf": (uni(0.75, 1.3, (512, 1)) / f_f[:, None]).astype(np.float32),
        "cd": np.tile(uni(0.75, 1.3, 512) / f_d, (128, 1)).astype(np.float32),
        "offs": striped(idx),
    }


def reference(xT, dyT, aT, w1, w2, gt, gam, cf, cd, offs):
    idx = unstriped(offs)
    x = f64(xT)[:, idx]
    dy = f64(dyT)[:, idx]
    a = f64(aT)[:, idx]
    gt_i = f64(gt)[:1][:, idx]
    dh = mxq(f64(w2), 0, "e4m3").T @ mxq(dy, 0, "e5m2")
    da = f64(cf) * gt_i * dh * sig(a) * (1.0 + a * (1.0 - sig(a)))
    dn = mxq(da, 0, "e5m2").T @ mxq(f64(w1), 0, "e4m3")
    xs = x.T
    xr = f64(cd)[:1] * xs
    s2 = (np.square(xr)).sum(-1, keepdims=True)
    rstd = 1.0 / np.sqrt(s2 / 512.0)
    n = xr * rstd
    h = f64(gam)[:1] * dn
    h2 = (h * n).sum(-1, keepdims=True)
    dx = f64(cd)[:1] * rstd * (h - n * h2 / 512.0)
    dxt = dx.T
    nd = dy + dxt
    out_0 = f64(dyT)
    out_0[:, idx] = nd
    return (out_0,) + planes(out_0)

@@ -1,0 +1,262 @@
+from contextlib import ExitStack
+
+import concourse.mybir as mybir
+from concourse.masks import make_identity
+
+P = 128
+PACK = 4
+D = 512
+F = 512
+T = 1024
+N = 512
+CH = N // P
+HALF = N // 2
+
+FLOPS = 2 * 2 * D * F * N
+
+F32 = mybir.dt.float32
+BF16 = mybir.dt.bfloat16
+U32 = mybir.dt.uint32
+I32 = mybir.dt.int32
+U16 = mybir.dt.uint16
+U8 = mybir.dt.uint8
+E4 = mybir.dt.float8_e4m3fn_x4
+E5 = mybir.dt.float8_e5m2_x4
+ALU = mybir.AluOpType
+ACT = mybir.ActivationFunctionType
+
+
+def tile_attend_gblock_sil_pl_kernel(tc, xT, dyT, aT, w1, w2, gt, gam, cf, cd, offs, out_0, out_1, out_2):
+    nc = tc.nc
+    with ExitStack() as ctx:
+        keep = ctx.enter_context(tc.tile_pool(name="keep", bufs=1))
+        ring = ctx.enter_context(tc.tile_pool(name="ring", bufs=2))
+        held = ctx.enter_context(tc.psum_pool(name="held", bufs=4))
+        turn = ctx.enter_context(tc.psum_pool(name="turn", bufs=4))
+
+        def planes(name, dtype=F32, width=T):
+            return [keep.tile([P, width], dtype, name="%s%d" % (name, j), align_bytes=64) for j in range(PACK)]
+
+        def rows(table):
+            return table.rearrange("(p j) t -> p j t", j=PACK)
+
+        def interleave(engine_copy, dst, src):
+            engine_copy(
+                dst.rearrange("p (c i t) -> p c t i", i=4, t=PACK),
+                src.rearrange("p t (c i) -> p c t i", i=4),
+            )
+
+        offsets = keep.tile([P, N // 16], U16, name="offsets")
+        nc.sync.dma_start(offsets[:], offs)
+        dy_win, a_win, x_win, out_win = planes("dy_win"), planes("a_win"), planes("x_win"), planes("out_win")
+        cd_col = keep.tile([P, PACK], F32)
+        gam_col = keep.tile([P, PACK], F32)
+        cf_col = keep.tile([P, PACK], F32)
+        ident = keep.tile([P, P], F32)
+        make_identity(nc, ident[:])
+        gt_win = keep.tile([P, T], F32)
+        nc.gpsimd.memset(gt_win[:], 0.0)
+        minus_half = keep.tile([P, CH], F32)
+        nc.gpsimd.memset(minus_half[:], -0.5)
+
+        w2_raw = keep.tile([P, PACK, F], F32)
+        w1_raw = keep.tile([P, PACK, D], F32)
+        nc.sync.dma_start(cd_col[:], cd[0:1, :].rearrange("o (p j) -> (o p) j", j=PACK))
+        nc.sync.dma_start(cf_col[:], cf.rearrange("(p j) o -> p (j o)", j=PACK))
+        for j in range(PACK):
+            nc.sync.dma_start(a_win[j][:], rows(aT)[:, j, :])
+        nc.sync.dma_start(gam_col[:], gam[0:1, :].rearrange("o (p j) -> (o p) j", j=PACK))
+        nc.sync.dma_start(gt_win[0:1, :], gt[0:1, :])
+        nc.sync.dma_start(w2_raw[:], rows(w2))
+        for j in range(PACK):
+            nc.sync.dma_start(dy_win[j][:], rows(dyT)[:, j, :])
+        nc.sync.dma_start(w1_raw[:], rows(w1))
+        for j in range(PACK):
+            nc.sync.dma_start(x_win[j][:], rows(xT)[:, j, :])
+        for j in range(PACK):
+            nc.sync.dma_start(out_win[j][:], rows(dyT)[:, j, :])
+
+        cf_half = keep.tile([P, PACK], F32)
+        cf_mhalf = keep.tile([P, PACK], F32)
+        nc.gpsimd.tensor_scalar(cf_half[:], cf_col[:], 0.5, 0.0, ALU.mult, ALU.add)
+        nc.gpsimd.tensor_scalar(cf_mhalf[:], cf_col[:], -0.5, 0.0, ALU.mult, ALU.add)
+        cd_wide = planes("cd_wide", F32, N)
+        for j in range(PACK):
+            nc.scalar.copy(cd_wide[j][:], cd_col[:, j : j + 1].to_broadcast([P, N]))
+        gam_ps = turn.tile([P, PACK, P], F32, tag="turn")
+        for j in range(PACK):
+            nc.tensor.transpose(gam_ps[:, j, :], gam_col[:, j : j + 1].to_broadcast([P, P]), ident[:])
+        gam_row = keep.tile([P, PACK, P], F32)
+        nc.scalar.copy(gam_row[:], gam_ps[:])
+
+        xs = planes("xs", F32, N)
+        for r in range(PACK):
+            a = keep.tile([P, N], F32, name="a%d" % r)
+            nc.vector.tensor_copy(a[:], a_win[r][:].indirect(offsets[:]))
+            silu = ring.tile([P, N], F32, tag="silu")
+            th = keep.tile([P, N], F32, name="th%d" % r)
+            lc = keep.tile([P, N], F32, name="lc%d" % r)
+            nc.scalar.activation(silu[:], a[:], ACT.Silu)
+            nc.scalar.activation(th[:], a[:], ACT.Tanh, scale=-0.5)
+            nc.scalar.activation(lc[:], silu[:], ACT.Identity, bias=cf_mhalf[:, r : r + 1], scale=cf_half[:, r : r + 1])
+            xs[r] = (xs[r], th, lc)
+
+        gt_g = keep.tile([P, N], F32)
+        nc.vector.tensor_copy(gt_g[:], gt_win[:].indirect(offsets[:]))
+        gt_ps = turn.tile([P, CH, P], F32, tag="turn")
+        for c in range(CH):
+            nc.tensor.transpose(gt_ps[:, c, :], gt_g[:, c * P : (c + 1) * P], ident[:])
+        gt_col = keep.tile([P, CH], F32)
+        nc.scalar.copy(gt_col[:], gt_ps[:, :, 0])
+
+        w2_bf = keep.tile([P, PACK * F], BF16, align_bytes=64)
+        interleave(nc.scalar.copy, w2_bf[:], w2_raw[:])
+        w2_q = keep.tile([P, F], U32, align_bytes=64)
+        w2_s = keep.tile([P, F], U8, align_bytes=64)
+        nc.vector.quantize_mx(w2_q[:].bitcast(E4), w2_s[:], w2_bf[:])
+
+        dy = keep.tile([P, PACK, N], F32)
+        for j in range(PACK):
+            nc.vector.tensor_copy(dy[:, j, :], dy_win[j][:].indirect(offsets[:]))
+        dy_bf = keep.tile([P, PACK * N], BF16, align_bytes=64)
+        interleave(nc.scalar.copy, dy_bf[:], dy[:])
+
+        for r in range(PACK):
+            x_r, th, lc = xs[r]
+            nc.vector.scalar_tensor_tensor(x_r[:], th[:], 1.0, lc[:], ALU.add, ALU.mult)
+
+        dy_q = keep.tile([P, N], U32, align_bytes=64)
+        dy_s = keep.tile([P, N], U8, align_bytes=64)
+        nc.vector.quantize_mx(dy_q[:].bitcast(E5), dy_s[:], dy_bf[:])
+        dhg = planes("dhg", F32, F)
+        for c in range(CH):
+            cols = slice(c * P, (c + 1) * P)
+            dh_ps = held.tile([P, F], F32, tag="held")
+            nc.tensor.matmul_mx(dh_ps[:], lhsT=dy_q[:, cols].bitcast(E5), lhsT_scale=dy_s[:, cols],
+                                rhs=w2_q[:].bitcast(E4), rhs_scale=w2_s[:], start=True, stop=True)
+            nc.scalar.activation(
+                dhg[c][:].rearrange("i (u p e) -> i u p e", u=2, e=2),
+                dh_ps[:].rearrange("i (p u e) -> i u p e", u=2, e=2),
+                ACT.Copy, scale=gt_col[:, c : c + 1])
+
+        xr = planes("xr", F32, N)
+        for j in range(PACK):
+            nc.vector.tensor_tensor(xr[j][:], x_win[j][:].indirect(offsets[:]), cd_wide[j][:], ALU.mult)
+        w1_bf = keep.tile([P, PACK * D], BF16, align_bytes=64)
+        interleave(nc.scalar.copy, w1_bf[:], w1_raw[:])
+        w1_q = keep.tile([P, D], U32, align_bytes=64)
+        w1_s = keep.tile([P, D], U8, align_bytes=64)
+        nc.vector.quantize_mx(w1_q[:].bitcast(E4), w1_s[:], w1_bf[:])
+
+        da_q = keep.tile([P, N], U32, align_bytes=64)
+        da_s = keep.tile([P, N], U8, align_bytes=64)
+        da_words = []
+        das = []
+        for c in range(CH):
+            cols = slice(c * P, (c + 1) * P)
+            g_ps = turn.tile([P, PACK, P], F32, tag="turn")
+            for r in range(PACK):
+                nc.tensor.matmul(g_ps[:, r, :], xs[r][0][:, cols], ident[:], start=True, stop=False, is_transpose=True)
+                nc.tensor.matmul(g_ps[:, r, :], cf_col[:, r : r + 1].to_broadcast([P, P]), ident[:],
+                                 start=False, stop=True, is_transpose=True)
+            da = keep.tile([P, F], BF16, name="da%d" % c, align_bytes=64)
+            nc.vector.tensor_tensor(
+                da[:].rearrange("i (u p e) -> i u p e", u=2, e=2),
+                g_ps[:].rearrange("i (u e) p -> i u p e", u=2),
+                dhg[c][:].rearrange("i (u p e) -> i u p e", u=2, e=2),
+                ALU.mult)
+            das.append(da)
+        for c in range(CH):
+            da = das[c]
+            w_ps = turn.tile([P, 2, P], F32, tag="turn")
+            for u in range(2):
+                nc.tensor.transpose(w_ps[:, u, :], da[:].bitcast(F32)[:, u * P : (u + 1) * P], ident[:])
+            da_t = keep.tile([P, F], BF16, name="da_t%d" % c, align_bytes=64)
+            nc.scalar.copy(da_t[:].bitcast(F32).rearrange("p (i u) -> p i u", u=2), w_ps[:].rearrange("p u i -> p i u"))
+            da_words.append(da_t)
+
+        ms = keep.tile([P, CH], F32)
+        xr_ps = []
+        for c in range(CH):
+            ps = held.tile([P, PACK, P], F32, tag="held", name="xr_ps%d" % c)
+            for j in range(PACK):
+                nc.tensor.transpose(ps[:, j, :], xr[j][:, c * P : (c + 1) * P], ident[:])
+            sq = ring.tile([P, D], BF16, tag="sq")
+            nc.scalar.activation(sq[:], ps[:].rearrange("i j p -> i (j p)"), ACT.Square, scale=D ** -0.5,
+                                 accum_out=ms[:, c : c + 1])
+            xr_ps.append(ps)
+        rstd = keep.tile([P, CH], F32)
+        r2 = keep.tile([P, CH], F32)
+        for half in range(2):
+            hc = slice(2 * half, 2 * half + 2)
+            nc.gpsimd.tensor_tensor(rstd[:, hc], ms[:, hc], minus_half[:, hc], ALU.pow)
+            nc.vector.scalar_tensor_tensor(r2[:, hc], rstd[:, hc], -1.0 / D, rstd[:, hc], ALU.mult, ALU.mult)
+
+        hs = planes("h", F32, D)
+        mm = planes("m", F32, D)
+        cc = keep.tile([P, CH], F32)
+        for c in range(CH):
+            cols = slice(c * P, (c + 1) * P)
+            nc.vector.quantize_mx(da_q[:, cols].bitcast(E5), da_s[:, cols], da_words[c][:])
+        dx = planes("dx", F32, N)
+        for half in range(2):
+            for c in (2 * half, 2 * half + 1):
+                cols = slice(c * P, (c + 1) * P)
+                dn_ps = turn.tile([P, D], F32, tag="turn")
+                nc.tensor.matmul_mx(dn_ps[:], lhsT=da_q[:, cols].bitcast(E5), lhsT_scale=da_s[:, cols],
+                                    rhs=w1_q[:].bitcast(E4), rhs_scale=w1_s[:], start=True, stop=True)
+                nc.vector.scalar_tensor_tensor(
+                    hs[c][:].rearrange("i (j p) -> i j p", j=PACK),
+                    dn_ps[:].rearrange("i (p j) -> i j p", j=PACK),
+                    rstd[:, c : c + 1], gam_row[:], ALU.mult, ALU.mult)
+            for c in (2 * half, 2 * half + 1):
+                xr_flat = xr_ps[c][:].rearrange("i j p -> i (j p)")
+                prod = ring.tile([P, D], F32, tag="prod")
+                nc.vector.scalar_tensor_tensor(prod[:], xr_flat, r2[:, c : c + 1], hs[c][:], ALU.mult, ALU.mult,
+                                               accum_out=cc[:, c : c + 1])
+                nc.scalar.activation(mm[c][:], xr_flat, ACT.Copy, scale=cc[:, c : c + 1])
+
+            for pair in range(2):
+                f_ps = turn.tile([P, 2, HALF], F32, tag="turn")
+                for e in range(2):
+                    j = 2 * pair + e
+                    for k in range(2):
+                        c = 2 * half + k
+                        dst = f_ps[:, e, k * P : (k + 1) * P]
+                        nc.tensor.matmul(dst, hs[c][:, j * P : (j + 1) * P], ident[:], start=True, stop=False, is_transpose=True)
+                        nc.tensor.matmul(dst, mm[c][:, j * P : (j + 1) * P], ident[:], start=False, stop=True, is_transpose=True)
+                for e in range(2):
+                    j = 2 * pair + e
+                    nc.scalar.activation(dx[j][:, half * HALF : (half + 1) * HALF], f_ps[:, e, :], ACT.Copy,
+                                         scale=cd_col[:, j : j + 1])
+
+        def scatter(j, lo, hi):
+            nc.vector.tensor_tensor(out_win[j][:].indirect(offsets[:, lo // 16 : hi // 16]),
+                                    dx[j][:, lo:hi], dy[:, j, lo:hi], ALU.add)
+
+        out_bf = keep.tile([P, T, PACK], BF16, align_bytes=64)
+        split = T // 2
+        scatter(0, 0, HALF)
+        scatter(1, 0, HALF)
+        for j in range(PACK):
+            if j < 2:
+                scatter(j, HALF, N)
+            else:
+                scatter(j, 0, N)
+            nc.sync.dma_start(rows(out_0)[:, j, :], out_win[j][:])
+            upto = T if j < 2 else split
+            nc.scalar.copy(out_bf[:, 0:upto, j], out_win[j][:, 0:upto])
+        for j in range(2, PACK):
+            nc.vector.tensor_copy(out_bf[:, split:T, j], out_win[j][:, split:T])
+
+        out_q = keep.tile([P, T], U32, align_bytes=64)
+        out_s = keep.tile([P, T], U8, align_bytes=64)
+        words = out_1.rearrange("a p c l -> p (a c l)").bitcast(I32)
+        for lo in (split, 0):
+            cols = slice(lo, lo + split)
+            nc.vector.quantize_mx(out_q[:, cols].bitcast(E4), out_s[:, cols],
+                                  out_bf[:, cols, :].rearrange("p c l -> p (c l)"))
+            nc.sync.dma_start(words[:, cols], out_q[:, cols].bitcast(I32))
+        scales = out_2.rearrange("a f c -> (a f) c").bitcast(I32)
+        for q in range(4):
+            nc.scalar.dma_start(scales[4 * q : 4 * q + 4, :], out_s[32 * q : 32 * q + 4, :].bitcast(I32))

@@ -52,12 +52,12 @@ def tile_attend_gblock_sil_pl_kernel(tc, xT, dyT, aT, w1, w2, gt, gam, cf, cd, o
         cd_col = keep.tile([P, PACK], F32)
         gam_col = keep.tile([P, PACK], F32)
         cf_col = keep.tile([P, PACK], F32)
+        one = keep.tile([P, 1], F32)
+        nc.gpsimd.memset(one[:], 1.0)
         ident = keep.tile([P, P], F32)
         make_identity(nc, ident[:])
         gt_win = keep.tile([P, T], F32)
         nc.gpsimd.memset(gt_win[:], 0.0)
-        minus_half = keep.tile([P, CH], F32)
-        nc.gpsimd.memset(minus_half[:], -0.5)
 
         w2_raw = keep.tile([P, PACK, F], F32)
         w1_raw = keep.tile([P, PACK, D], F32)
@@ -67,8 +67,9 @@ def tile_attend_gblock_sil_pl_kernel(tc, xT, dyT, aT, w1, w2, gt, gam, cf, cd, o
             nc.sync.dma_start(a_win[j][:], rows(aT)[:, j, :])
         nc.sync.dma_start(gam_col[:], gam[0:1, :].rearrange("o (p j) -> (o p) j", j=PACK))
         nc.sync.dma_start(gt_win[0:1, :], gt[0:1, :])
-        nc.sync.dma_start(w2_raw[:], rows(w2))
         for j in range(PACK):
+            if j == 2:
+                nc.sync.dma_start(w2_raw[:], rows(w2))
             nc.sync.dma_start(dy_win[j][:], rows(dyT)[:, j, :])
         nc.sync.dma_start(w1_raw[:], rows(w1))
         for j in range(PACK):
@@ -76,6 +77,8 @@ def tile_attend_gblock_sil_pl_kernel(tc, xT, dyT, aT, w1, w2, gt, gam, cf, cd, o
         for j in range(PACK):
             nc.sync.dma_start(out_win[j][:], rows(dyT)[:, j, :])
 
+        warm = keep.tile([P, 1], F32)
+        nc.scalar.activation(warm[:], one[:], ACT.Silu)
         cf_half = keep.tile([P, PACK], F32)
         cf_mhalf = keep.tile([P, PACK], F32)
         nc.gpsimd.tensor_scalar(cf_half[:], cf_col[:], 0.5, 0.0, ALU.mult, ALU.add)
@@ -89,17 +92,15 @@ def tile_attend_gblock_sil_pl_kernel(tc, xT, dyT, aT, w1, w2, gt, gam, cf, cd, o
         gam_row = keep.tile([P, PACK, P], F32)
         nc.scalar.copy(gam_row[:], gam_ps[:])
 
-        xs = planes("xs", F32, N)
+        th = keep.tile([P, PACK, N], F32)
+        lc = keep.tile([P, PACK, N], F32)
         for r in range(PACK):
             a = keep.tile([P, N], F32, name="a%d" % r)
             nc.vector.tensor_copy(a[:], a_win[r][:].indirect(offsets[:]))
             silu = ring.tile([P, N], F32, tag="silu")
-            th = keep.tile([P, N], F32, name="th%d" % r)
-            lc = keep.tile([P, N], F32, name="lc%d" % r)
             nc.scalar.activation(silu[:], a[:], ACT.Silu)
-            nc.scalar.activation(th[:], a[:], ACT.Tanh, scale=-0.5)
-            nc.scalar.activation(lc[:], silu[:], ACT.Identity, bias=cf_mhalf[:, r : r + 1], scale=cf_half[:, r : r + 1])
-            xs[r] = (xs[r], th, lc)
+            nc.scalar.activation(th[:, r, :], a[:], ACT.Tanh, scale=-0.5)
+            nc.scalar.activation(lc[:, r, :], silu[:], ACT.Identity, bias=cf_mhalf[:, r : r + 1], scale=cf_half[:, r : r + 1])
 
         gt_g = keep.tile([P, N], F32)
         nc.vector.tensor_copy(gt_g[:], gt_win[:].indirect(offsets[:]))
@@ -121,13 +122,21 @@ def tile_attend_gblock_sil_pl_kernel(tc, xT, dyT, aT, w1, w2, gt, gam, cf, cd, o
         dy_bf = keep.tile([P, PACK * N], BF16, align_bytes=64)
         interleave(nc.scalar.copy, dy_bf[:], dy[:])
 
-        for r in range(PACK):
-            x_r, th, lc = xs[r]
-            nc.vector.scalar_tensor_tensor(x_r[:], th[:], 1.0, lc[:], ALU.add, ALU.mult)
-
         dy_q = keep.tile([P, N], U32, align_bytes=64)
         dy_s = keep.tile([P, N], U8, align_bytes=64)
         nc.vector.quantize_mx(dy_q[:].bitcast(E5), dy_s[:], dy_bf[:])
+        gm = keep.tile([P, PACK, N], F32, tag="dy_win3", align_bytes=64)
+        nc.vector.scalar_tensor_tensor(gm[:], th[:], 1.0, lc[:], ALU.add, ALU.mult)
+
+        g_banks = []
+        for c in range(CH):
+            cols = slice(c * P, (c + 1) * P)
+            g_ps = turn.tile([P, PACK, P], F32, tag="turn")
+            for r in range(PACK):
+                nc.tensor.matmul(g_ps[:, r, :], gm[:, r, cols], ident[:], start=True, stop=False, is_transpose=True)
+                nc.tensor.matmul(g_ps[:, r, :], cf_col[:, r : r + 1].to_broadcast([P, P]), ident[:],
+                                 start=False, stop=True, is_transpose=True)
+            g_banks.append(g_ps)
         dhg = planes("dhg", F32, F)
         for c in range(CH):
             cols = slice(c * P, (c + 1) * P)
@@ -148,17 +157,36 @@ def tile_attend_gblock_sil_pl_kernel(tc, xT, dyT, aT, w1, w2, gt, gam, cf, cd, o
         w1_s = keep.tile([P, D], U8, align_bytes=64)
         nc.vector.quantize_mx(w1_q[:].bitcast(E4), w1_s[:], w1_bf[:])
 
+        warm_sqrt = keep.tile([P, 1], F32)
+        nc.scalar.activation(warm_sqrt[:], w1_bf[:, 0:1], ACT.Sqrt, bias=one[:], scale=0.0)
+        ms = keep.tile([P, CH], F32)
+        rstd = keep.tile([P, CH], F32)
+        std = keep.tile([P, CH], F32)
+        r2 = keep.tile([P, CH], F32)
+        xr_ps = []
+
+        def norm(half):
+            for c in (2 * half, 2 * half + 1):
+                ps = held.tile([P, PACK, P], F32, tag="held", name="xr_ps%d" % c)
+                for j in range(PACK):
+                    nc.tensor.transpose(ps[:, j, :], xr[j][:, c * P : (c + 1) * P], ident[:])
+                sq = ring.tile([P, D], BF16, tag="sq")
+                nc.scalar.activation(sq[:], ps[:].rearrange("i j p -> i (j p)"), ACT.Square, scale=D ** -0.5,
+                                     accum_out=ms[:, c : c + 1])
+                xr_ps.append(ps)
+            hc = slice(2 * half, 2 * half + 2)
+            nc.scalar.activation(std[:, hc], ms[:, hc], ACT.Sqrt)
+            nc.vector.reciprocal(rstd[:, hc], std[:, hc])
+            nc.vector.scalar_tensor_tensor(r2[:, hc], rstd[:, hc], -1.0 / D, rstd[:, hc], ALU.mult, ALU.mult)
+
+        norm(0)
         da_q = keep.tile([P, N], U32, align_bytes=64)
         da_s = keep.tile([P, N], U8, align_bytes=64)
         da_words = []
         das = []
         for c in range(CH):
             cols = slice(c * P, (c + 1) * P)
-            g_ps = turn.tile([P, PACK, P], F32, tag="turn")
-            for r in range(PACK):
-                nc.tensor.matmul(g_ps[:, r, :], xs[r][0][:, cols], ident[:], start=True, stop=False, is_transpose=True)
-                nc.tensor.matmul(g_ps[:, r, :], cf_col[:, r : r + 1].to_broadcast([P, P]), ident[:],
-                                 start=False, stop=True, is_transpose=True)
+            g_ps = g_banks[c]
             da = keep.tile([P, F], BF16, name="da%d" % c, align_bytes=64)
             nc.vector.tensor_tensor(
                 da[:].rearrange("i (u p e) -> i u p e", u=2, e=2),
@@ -175,22 +203,7 @@ def tile_attend_gblock_sil_pl_kernel(tc, xT, dyT, aT, w1, w2, gt, gam, cf, cd, o
             nc.scalar.copy(da_t[:].bitcast(F32).rearrange("p (i u) -> p i u", u=2), w_ps[:].rearrange("p u i -> p i u"))
             da_words.append(da_t)
 
-        ms = keep.tile([P, CH], F32)
-        xr_ps = []
-        for c in range(CH):
-            ps = held.tile([P, PACK, P], F32, tag="held", name="xr_ps%d" % c)
-            for j in range(PACK):
-                nc.tensor.transpose(ps[:, j, :], xr[j][:, c * P : (c + 1) * P], ident[:])
-            sq = ring.tile([P, D], BF16, tag="sq")
-            nc.scalar.activation(sq[:], ps[:].rearrange("i j p -> i (j p)"), ACT.Square, scale=D ** -0.5,
-                                 accum_out=ms[:, c : c + 1])
-            xr_ps.append(ps)
-        rstd = keep.tile([P, CH], F32)
-        r2 = keep.tile([P, CH], F32)
-        for half in range(2):
-            hc = slice(2 * half, 2 * half + 2)
-            nc.gpsimd.tensor_tensor(rstd[:, hc], ms[:, hc], minus_half[:, hc], ALU.pow)
-            nc.vector.scalar_tensor_tensor(r2[:, hc], rstd[:, hc], -1.0 / D, rstd[:, hc], ALU.mult, ALU.mult)
+        norm(1)
 
         hs = planes("h", F32, D)
         mm = planes("m", F32, D)
@@ -259,4 +272,5 @@ def tile_attend_gblock_sil_pl_kernel(tc, xT, dyT, aT, w1, w2, gt, gam, cf, cd, o
             nc.sync.dma_start(words[:, cols], out_q[:, cols].bitcast(I32))
         scales = out_2.rearrange("a f c -> (a f) c").bitcast(I32)
         for q in range(4):
-            nc.scalar.dma_start(scales[4 * q : 4 * q + 4, :], out_s[32 * q : 32 * q + 4, :].bitcast(I32))
+            queue = nc.sync if q % 2 else nc.scalar
+            queue.dma_start(scales[4 * q : 4 * q + 4, :], out_s[32 * q : 32 * q + 4, :].bitcast(I32))

@@ -57,7 +57,7 @@ def tile_attend_gblock_sil_pl_kernel(tc, xT, dyT, aT, w1, w2, gt, gam, cf, cd, o
         ident = keep.tile([P, P], F32)
         make_identity(nc, ident[:])
         gt_win = keep.tile([P, T], F32)
-        nc.gpsimd.memset(gt_win[:], 0.0)
+        nc.vector.memset(gt_win[:], 0.0)
 
         w2_raw = keep.tile([P, PACK, F], F32)
         w1_raw = keep.tile([P, PACK, D], F32)
@@ -71,8 +71,9 @@ def tile_attend_gblock_sil_pl_kernel(tc, xT, dyT, aT, w1, w2, gt, gam, cf, cd, o
             if j == 2:
                 nc.sync.dma_start(w2_raw[:], rows(w2))
             nc.sync.dma_start(dy_win[j][:], rows(dyT)[:, j, :])
-        nc.sync.dma_start(w1_raw[:], rows(w1))
         for j in range(PACK):
+            if j == 2:
+                nc.sync.dma_start(w1_raw[:], rows(w1))
             nc.sync.dma_start(x_win[j][:], rows(xT)[:, j, :])
         for j in range(PACK):
             nc.sync.dma_start(out_win[j][:], rows(dyT)[:, j, :])
@@ -86,7 +87,7 @@ def tile_attend_gblock_sil_pl_kernel(tc, xT, dyT, aT, w1, w2, gt, gam, cf, cd, o
         cd_wide = planes("cd_wide", F32, N)
         for j in range(PACK):
             nc.scalar.copy(cd_wide[j][:], cd_col[:, j : j + 1].to_broadcast([P, N]))
-        gam_ps = turn.tile([P, PACK, P], F32, tag="turn")
+        gam_ps = held.tile([P, PACK, P], F32, tag="held")
         for j in range(PACK):
             nc.tensor.transpose(gam_ps[:, j, :], gam_col[:, j : j + 1].to_broadcast([P, P]), ident[:])
         gam_row = keep.tile([P, PACK, P], F32)
@@ -94,17 +95,19 @@ def tile_attend_gblock_sil_pl_kernel(tc, xT, dyT, aT, w1, w2, gt, gam, cf, cd, o
 
         th = keep.tile([P, PACK, N], F32)
         lc = keep.tile([P, PACK, N], F32)
+        gm = keep.tile([P, PACK, N], F32)
         for r in range(PACK):
             a = keep.tile([P, N], F32, name="a%d" % r)
             nc.vector.tensor_copy(a[:], a_win[r][:].indirect(offsets[:]))
-            silu = ring.tile([P, N], F32, tag="silu")
+            silu = ring.tile([P, N], F32, tag="silu", bufs=3)
             nc.scalar.activation(silu[:], a[:], ACT.Silu)
             nc.scalar.activation(th[:, r, :], a[:], ACT.Tanh, scale=-0.5)
-            nc.scalar.activation(lc[:, r, :], silu[:], ACT.Identity, bias=cf_mhalf[:, r : r + 1], scale=cf_half[:, r : r + 1])
+            nc.gpsimd.tensor_scalar(lc[:, r, :], silu[:], cf_half[:, r : r + 1], cf_mhalf[:, r : r + 1], ALU.mult, ALU.add)
+            nc.gpsimd.tensor_tensor(gm[:, r, :], lc[:, r, :], th[:, r, :], ALU.mult)
 
         gt_g = keep.tile([P, N], F32)
         nc.vector.tensor_copy(gt_g[:], gt_win[:].indirect(offsets[:]))
-        gt_ps = turn.tile([P, CH, P], F32, tag="turn")
+        gt_ps = held.tile([P, CH, P], F32, tag="held")
         for c in range(CH):
             nc.tensor.transpose(gt_ps[:, c, :], gt_g[:, c * P : (c + 1) * P], ident[:])
         gt_col = keep.tile([P, CH], F32)
@@ -125,17 +128,18 @@ def tile_attend_gblock_sil_pl_kernel(tc, xT, dyT, aT, w1, w2, gt, gam, cf, cd, o
         dy_q = keep.tile([P, N], U32, align_bytes=64)
         dy_s = keep.tile([P, N], U8, align_bytes=64)
         nc.vector.quantize_mx(dy_q[:].bitcast(E5), dy_s[:], dy_bf[:])
-        gm = keep.tile([P, PACK, N], F32, tag="dy_win3", align_bytes=64)
-        nc.vector.scalar_tensor_tensor(gm[:], th[:], 1.0, lc[:], ALU.add, ALU.mult)
 
         g_banks = []
         for c in range(CH):
             cols = slice(c * P, (c + 1) * P)
             g_ps = turn.tile([P, PACK, P], F32, tag="turn")
             for r in range(PACK):
-                nc.tensor.matmul(g_ps[:, r, :], gm[:, r, cols], ident[:], start=True, stop=False, is_transpose=True)
                 nc.tensor.matmul(g_ps[:, r, :], cf_col[:, r : r + 1].to_broadcast([P, P]), ident[:],
-                                 start=False, stop=True, is_transpose=True)
+                                 start=(r == 0), stop=False, is_transpose=True)
+            for r in range(PACK):
+                nc.tensor.matmul(g_ps[:, r, :], lc[:, r, cols], ident[:], start=False, stop=False, is_transpose=True)
+            for r in range(PACK):
+                nc.tensor.matmul(g_ps[:, r, :], gm[:, r, cols], ident[:], start=False, stop=(r == PACK - 1), is_transpose=True)
             g_banks.append(g_ps)
         dhg = planes("dhg", F32, F)
         for c in range(CH):
@@ -158,7 +162,7 @@ def tile_attend_gblock_sil_pl_kernel(tc, xT, dyT, aT, w1, w2, gt, gam, cf, cd, o
         nc.vector.quantize_mx(w1_q[:].bitcast(E4), w1_s[:], w1_bf[:])
 
         warm_sqrt = keep.tile([P, 1], F32)
-        nc.scalar.activation(warm_sqrt[:], w1_bf[:, 0:1], ACT.Sqrt, bias=one[:], scale=0.0)
+        nc.scalar.activation(warm_sqrt[:], w2_bf[:, 0:1], ACT.Sqrt, bias=one[:], scale=0.0)
         ms = keep.tile([P, CH], F32)
         rstd = keep.tile([P, CH], F32)
         std = keep.tile([P, CH], F32)
@@ -231,13 +235,11 @@ def tile_attend_gblock_sil_pl_kernel(tc, xT, dyT, aT, w1, w2, gt, gam, cf, cd, o
 
             for pair in range(2):
                 f_ps = turn.tile([P, 2, HALF], F32, tag="turn")
-                for e in range(2):
+                parts = [(src, k, e) for src in (hs, mm) for k in range(2) for e in range(2)]
+                for n, (src, k, e) in enumerate(parts):
                     j = 2 * pair + e
-                    for k in range(2):
-                        c = 2 * half + k
-                        dst = f_ps[:, e, k * P : (k + 1) * P]
-                        nc.tensor.matmul(dst, hs[c][:, j * P : (j + 1) * P], ident[:], start=True, stop=False, is_transpose=True)
-                        nc.tensor.matmul(dst, mm[c][:, j * P : (j + 1) * P], ident[:], start=False, stop=True, is_transpose=True)
+                    nc.tensor.matmul(f_ps[:, e, k * P : (k + 1) * P], src[2 * half + k][:, j * P : (j + 1) * P], ident[:],
+                                     start=(n == 0), stop=(n == len(parts) - 1), is_transpose=True)
                 for e in range(2):
                     j = 2 * pair + e
                     nc.scalar.activation(dx[j][:, half * HALF : (half + 1) * HALF], f_ps[:, e, :], ACT.Copy,
@@ -258,15 +260,16 @@ def tile_attend_gblock_sil_pl_kernel(tc, xT, dyT, aT, w1, w2, gt, gam, cf, cd, o
                 scatter(j, 0, N)
             nc.sync.dma_start(rows(out_0)[:, j, :], out_win[j][:])
             upto = T if j < 2 else split
-            nc.scalar.copy(out_bf[:, 0:upto, j], out_win[j][:, 0:upto])
+            for lo, hi in ((0, upto),) if j < PACK - 1 else ((0, upto // 2), (upto // 2, upto)):
+                nc.scalar.copy(out_bf[:, lo:hi, j], out_win[j][:, lo:hi])
         for j in range(2, PACK):
             nc.vector.tensor_copy(out_bf[:, split:T, j], out_win[j][:, split:T])
 
         out_q = keep.tile([P, T], U32, align_bytes=64)
         out_s = keep.tile([P, T], U8, align_bytes=64)
         words = out_1.rearrange("a p c l -> p (a c l)").bitcast(I32)
-        for lo in (split, 0):
-            cols = slice(lo, lo + split)
+        for lo, hi in ((split, T), (0, split // 2), (split // 2, split)):
+            cols = slice(lo, hi)
             nc.vector.quantize_mx(out_q[:, cols].bitcast(E4), out_s[:, cols],
                                   out_bf[:, cols, :].rearrange("p c l -> p (c l)"))
             nc.sync.dma_start(words[:, cols], out_q[:, cols].bitcast(I32))

@@ -102,7 +102,10 @@ def tile_attend_gblock_sil_pl_kernel(tc, xT, dyT, aT, w1, w2, gt, gam, cf, cd, o
             silu = ring.tile([P, N], F32, tag="silu", bufs=3)
             nc.scalar.activation(silu[:], a[:], ACT.Silu)
             nc.scalar.activation(th[:, r, :], a[:], ACT.Tanh, scale=-0.5)
-            nc.gpsimd.tensor_scalar(lc[:, r, :], silu[:], cf_half[:, r : r + 1], cf_mhalf[:, r : r + 1], ALU.mult, ALU.add)
+            if r < 2:
+                nc.gpsimd.tensor_scalar(lc[:, r, :], silu[:], cf_half[:, r : r + 1], cf_mhalf[:, r : r + 1], ALU.mult, ALU.add)
+            else:
+                nc.scalar.activation(lc[:, r, :], silu[:], ACT.Identity, bias=cf_mhalf[:, r : r + 1], scale=cf_half[:, r : r + 1])
             nc.gpsimd.tensor_tensor(gm[:, r, :], lc[:, r, :], th[:, r, :], ALU.mult)
 
         gt_g = keep.tile([P, N], F32)

@@ -9,8 +9,11 @@ D = 512
 F = 512
 T = 1024
 N = 512
-CH = N // P
+CHUNKS = N // P
 HALF = N // 2
+LIST_ROWS = 16
+GPSIMD_AFFINES = 2
+SCALAR_TOKENS = T // 2
 
 FLOPS = 2 * 2 * D * F * N
 
@@ -20,8 +23,8 @@ U32 = mybir.dt.uint32
 I32 = mybir.dt.int32
 U16 = mybir.dt.uint16
 U8 = mybir.dt.uint8
-E4 = mybir.dt.float8_e4m3fn_x4
-E5 = mybir.dt.float8_e5m2_x4
+E4M3 = mybir.dt.float8_e4m3fn_x4
+E5M2 = mybir.dt.float8_e5m2_x4
 ALU = mybir.AluOpType
 ACT = mybir.ActivationFunctionType
 
@@ -31,13 +34,13 @@ def tile_attend_gblock_sil_pl_kernel(tc, xT, dyT, aT, w1, w2, gt, gam, cf, cd, o
     with ExitStack() as ctx:
         keep = ctx.enter_context(tc.tile_pool(name="keep", bufs=1))
         ring = ctx.enter_context(tc.tile_pool(name="ring", bufs=2))
-        held = ctx.enter_context(tc.psum_pool(name="held", bufs=4))
-        turn = ctx.enter_context(tc.psum_pool(name="turn", bufs=4))
+        held = ctx.enter_context(tc.psum_pool(name="held", bufs=CHUNKS))
+        turn = ctx.enter_context(tc.psum_pool(name="turn", bufs=CHUNKS))
 
-        def planes(name, dtype=F32, width=T):
-            return [keep.tile([P, width], dtype, name="%s%d" % (name, j), align_bytes=64) for j in range(PACK)]
+        def four_tiles(name, width):
+            return [keep.tile([P, width], F32, name="%s%d" % (name, j), align_bytes=64) for j in range(PACK)]
 
-        def rows(table):
+        def by_planes(table):
             return table.rearrange("(p j) t -> p j t", j=PACK)
 
         def interleave(engine_copy, dst, src):
@@ -46,9 +49,16 @@ def tile_attend_gblock_sil_pl_kernel(tc, xT, dyT, aT, w1, w2, gt, gam, cf, cd, o
                 src.rearrange("p t (c i) -> p c t i", i=4),
             )
 
-        offsets = keep.tile([P, N // 16], U16, name="offsets")
+        def chunk_slots(c):
+            return slice(c * P, (c + 1) * P)
+
+        def listed(window, lo=0, hi=N):
+            return window[:].indirect(offsets[:, lo // LIST_ROWS : hi // LIST_ROWS])
+
+        offsets = keep.tile([P, N // LIST_ROWS], U16, name="offsets")
         nc.sync.dma_start(offsets[:], offs)
-        dy_win, a_win, x_win, out_win = planes("dy_win"), planes("a_win"), planes("x_win"), planes("out_win")
+        dy_win, a_win = four_tiles("dy_win", T), four_tiles("a_win", T)
+        x_win, out_win = four_tiles("x_win", T), four_tiles("out_win", T)
         cd_col = keep.tile([P, PACK], F32)
         gam_col = keep.tile([P, PACK], F32)
         cf_col = keep.tile([P, PACK], F32)
@@ -60,31 +70,31 @@ def tile_attend_gblock_sil_pl_kernel(tc, xT, dyT, aT, w1, w2, gt, gam, cf, cd, o
         nc.vector.memset(gt_win[:], 0.0)
 
         w2_raw = keep.tile([P, PACK, F], F32)
-        w1_raw = keep.tile([P, PACK, D], F32)
+        w1_raw = [keep.tile([P, PACK, D // 2], F32, name="w1_raw%d" % u) for u in range(2)]
         nc.sync.dma_start(cd_col[:], cd[0:1, :].rearrange("o (p j) -> (o p) j", j=PACK))
         nc.sync.dma_start(cf_col[:], cf.rearrange("(p j) o -> p (j o)", j=PACK))
         for j in range(PACK):
-            nc.sync.dma_start(a_win[j][:], rows(aT)[:, j, :])
+            nc.sync.dma_start(a_win[j][:], by_planes(aT)[:, j, :])
         nc.sync.dma_start(gam_col[:], gam[0:1, :].rearrange("o (p j) -> (o p) j", j=PACK))
         nc.sync.dma_start(gt_win[0:1, :], gt[0:1, :])
         for j in range(PACK):
-            if j == 2:
-                nc.sync.dma_start(w2_raw[:], rows(w2))
-            nc.sync.dma_start(dy_win[j][:], rows(dyT)[:, j, :])
+            nc.sync.dma_start(dy_win[j][:], by_planes(dyT)[:, j, :])
+        nc.sync.dma_start(w2_raw[:], by_planes(w2))
         for j in range(PACK):
-            if j == 2:
-                nc.sync.dma_start(w1_raw[:], rows(w1))
-            nc.sync.dma_start(x_win[j][:], rows(xT)[:, j, :])
+            nc.sync.dma_start(x_win[j][:], by_planes(xT)[:, j, :])
+        for u in range(2):
+            nc.sync.dma_start(w1_raw[u][:], by_planes(w1)[:, :, u * (D // 2) : (u + 1) * (D // 2)])
         for j in range(PACK):
-            nc.sync.dma_start(out_win[j][:], rows(dyT)[:, j, :])
+            nc.sync.dma_start(out_win[j][:], by_planes(dyT)[:, j, :])
 
-        warm = keep.tile([P, 1], F32)
-        nc.scalar.activation(warm[:], one[:], ACT.Silu)
+        warm_silu = keep.tile([P, 1], F32)
+        nc.scalar.activation(warm_silu[:], one[:], ACT.Silu)
+
         cf_half = keep.tile([P, PACK], F32)
-        cf_mhalf = keep.tile([P, PACK], F32)
+        cf_minus_half = keep.tile([P, PACK], F32)
         nc.gpsimd.tensor_scalar(cf_half[:], cf_col[:], 0.5, 0.0, ALU.mult, ALU.add)
-        nc.gpsimd.tensor_scalar(cf_mhalf[:], cf_col[:], -0.5, 0.0, ALU.mult, ALU.add)
-        cd_wide = planes("cd_wide", F32, N)
+        nc.gpsimd.tensor_scalar(cf_minus_half[:], cf_col[:], -0.5, 0.0, ALU.mult, ALU.add)
+        cd_wide = four_tiles("cd_wide", N)
         for j in range(PACK):
             nc.scalar.copy(cd_wide[j][:], cd_col[:, j : j + 1].to_broadcast([P, N]))
         gam_ps = held.tile([P, PACK, P], F32, tag="held")
@@ -93,190 +103,190 @@ def tile_attend_gblock_sil_pl_kernel(tc, xT, dyT, aT, w1, w2, gt, gam, cf, cd, o
         gam_row = keep.tile([P, PACK, P], F32)
         nc.scalar.copy(gam_row[:], gam_ps[:])
 
-        th = keep.tile([P, PACK, N], F32)
-        lc = keep.tile([P, PACK, N], F32)
-        gm = keep.tile([P, PACK, N], F32)
-        for r in range(PACK):
-            a = keep.tile([P, N], F32, name="a%d" % r)
-            nc.vector.tensor_copy(a[:], a_win[r][:].indirect(offsets[:]))
+        tanh = keep.tile([P, PACK, N], F32)
+        affine = keep.tile([P, PACK, N], F32)
+        cross = keep.tile([P, PACK, N], F32)
+        for j in range(PACK):
+            a = keep.tile([P, N], F32, name="a%d" % j)
+            nc.vector.tensor_copy(a[:], listed(a_win[j]))
             silu = ring.tile([P, N], F32, tag="silu", bufs=3)
             nc.scalar.activation(silu[:], a[:], ACT.Silu)
-            nc.scalar.activation(th[:, r, :], a[:], ACT.Tanh, scale=-0.5)
-            if r < 2:
-                nc.gpsimd.tensor_scalar(lc[:, r, :], silu[:], cf_half[:, r : r + 1], cf_mhalf[:, r : r + 1], ALU.mult, ALU.add)
+            nc.scalar.activation(tanh[:, j, :], a[:], ACT.Tanh, scale=-0.5)
+            factor, shift = cf_half[:, j : j + 1], cf_minus_half[:, j : j + 1]
+            if j < GPSIMD_AFFINES:
+                nc.gpsimd.tensor_scalar(affine[:, j, :], silu[:], factor, shift, ALU.mult, ALU.add)
             else:
-                nc.scalar.activation(lc[:, r, :], silu[:], ACT.Identity, bias=cf_mhalf[:, r : r + 1], scale=cf_half[:, r : r + 1])
-            nc.gpsimd.tensor_tensor(gm[:, r, :], lc[:, r, :], th[:, r, :], ALU.mult)
+                nc.scalar.activation(affine[:, j, :], silu[:], ACT.Identity, bias=shift, scale=factor)
+            nc.gpsimd.tensor_tensor(cross[:, j, :], affine[:, j, :], tanh[:, j, :], ALU.mult)
 
-        gt_g = keep.tile([P, N], F32)
-        nc.vector.tensor_copy(gt_g[:], gt_win[:].indirect(offsets[:]))
-        gt_ps = held.tile([P, CH, P], F32, tag="held")
-        for c in range(CH):
-            nc.tensor.transpose(gt_ps[:, c, :], gt_g[:, c * P : (c + 1) * P], ident[:])
-        gt_col = keep.tile([P, CH], F32)
+        gt_row = keep.tile([P, N], F32)
+        nc.vector.tensor_copy(gt_row[:], listed(gt_win))
+        gt_ps = held.tile([P, CHUNKS, P], F32, tag="held")
+        for c in range(CHUNKS):
+            nc.tensor.transpose(gt_ps[:, c, :], gt_row[:, chunk_slots(c)], ident[:])
+        gt_col = keep.tile([P, CHUNKS], F32)
         nc.scalar.copy(gt_col[:], gt_ps[:, :, 0])
 
         w2_bf = keep.tile([P, PACK * F], BF16, align_bytes=64)
-        interleave(nc.scalar.copy, w2_bf[:], w2_raw[:])
-        w2_q = keep.tile([P, F], U32, align_bytes=64)
-        w2_s = keep.tile([P, F], U8, align_bytes=64)
-        nc.vector.quantize_mx(w2_q[:].bitcast(E4), w2_s[:], w2_bf[:])
+        interleave(nc.vector.tensor_copy, w2_bf[:], w2_raw[:])
+        w2_codes = keep.tile([P, F], U32, align_bytes=64)
+        w2_scales = keep.tile([P, F], U8, align_bytes=64)
+        nc.vector.quantize_mx(w2_codes[:].bitcast(E4M3), w2_scales[:], w2_bf[:])
 
         dy = keep.tile([P, PACK, N], F32)
         for j in range(PACK):
-            nc.vector.tensor_copy(dy[:, j, :], dy_win[j][:].indirect(offsets[:]))
+            nc.vector.tensor_copy(dy[:, j, :], listed(dy_win[j]))
         dy_bf = keep.tile([P, PACK * N], BF16, align_bytes=64)
         interleave(nc.scalar.copy, dy_bf[:], dy[:])
+        dy_codes = keep.tile([P, N], U32, align_bytes=64)
+        dy_scales = keep.tile([P, N], U8, align_bytes=64)
+        nc.vector.quantize_mx(dy_codes[:].bitcast(E5M2), dy_scales[:], dy_bf[:])
 
-        dy_q = keep.tile([P, N], U32, align_bytes=64)
-        dy_s = keep.tile([P, N], U8, align_bytes=64)
-        nc.vector.quantize_mx(dy_q[:].bitcast(E5), dy_s[:], dy_bf[:])
+        slope_ps = []
+        for c in range(CHUNKS):
+            bank = turn.tile([P, PACK, P], F32, tag="turn")
+            for j in range(PACK):
+                nc.tensor.matmul(bank[:, j, :], cf_col[:, j : j + 1].to_broadcast([P, P]), ident[:],
+                                 start=(j == 0), stop=False, is_transpose=True)
+            for j in range(PACK):
+                nc.tensor.matmul(bank[:, j, :], affine[:, j, chunk_slots(c)], ident[:],
+                                 start=False, stop=False, is_transpose=True)
+            for j in range(PACK):
+                nc.tensor.matmul(bank[:, j, :], cross[:, j, chunk_slots(c)], ident[:],
+                                 start=False, stop=(j == PACK - 1), is_transpose=True)
+            slope_ps.append(bank)
 
-        g_banks = []
-        for c in range(CH):
-            cols = slice(c * P, (c + 1) * P)
-            g_ps = turn.tile([P, PACK, P], F32, tag="turn")
-            for r in range(PACK):
-                nc.tensor.matmul(g_ps[:, r, :], cf_col[:, r : r + 1].to_broadcast([P, P]), ident[:],
-                                 start=(r == 0), stop=False, is_transpose=True)
-            for r in range(PACK):
-                nc.tensor.matmul(g_ps[:, r, :], lc[:, r, cols], ident[:], start=False, stop=False, is_transpose=True)
-            for r in range(PACK):
-                nc.tensor.matmul(g_ps[:, r, :], gm[:, r, cols], ident[:], start=False, stop=(r == PACK - 1), is_transpose=True)
-            g_banks.append(g_ps)
-        dhg = planes("dhg", F32, F)
-        for c in range(CH):
-            cols = slice(c * P, (c + 1) * P)
+        dh_gated = four_tiles("dh_gated", F)
+        for c in range(CHUNKS):
             dh_ps = held.tile([P, F], F32, tag="held")
-            nc.tensor.matmul_mx(dh_ps[:], lhsT=dy_q[:, cols].bitcast(E5), lhsT_scale=dy_s[:, cols],
-                                rhs=w2_q[:].bitcast(E4), rhs_scale=w2_s[:], start=True, stop=True)
+            nc.tensor.matmul_mx(dh_ps[:], lhsT=dy_codes[:, chunk_slots(c)].bitcast(E5M2),
+                                lhsT_scale=dy_scales[:, chunk_slots(c)],
+                                rhs=w2_codes[:].bitcast(E4M3), rhs_scale=w2_scales[:], start=True, stop=True)
             nc.scalar.activation(
-                dhg[c][:].rearrange("i (u p e) -> i u p e", u=2, e=2),
+                dh_gated[c][:].rearrange("i (u p e) -> i u p e", u=2, e=2),
                 dh_ps[:].rearrange("i (p u e) -> i u p e", u=2, e=2),
                 ACT.Copy, scale=gt_col[:, c : c + 1])
 
-        xr = planes("xr", F32, N)
+        xr = four_tiles("xr", N)
         for j in range(PACK):
-            nc.vector.tensor_tensor(xr[j][:], x_win[j][:].indirect(offsets[:]), cd_wide[j][:], ALU.mult)
+            nc.vector.tensor_tensor(xr[j][:], listed(x_win[j]), cd_wide[j][:], ALU.mult)
+
         w1_bf = keep.tile([P, PACK * D], BF16, align_bytes=64)
-        interleave(nc.scalar.copy, w1_bf[:], w1_raw[:])
-        w1_q = keep.tile([P, D], U32, align_bytes=64)
-        w1_s = keep.tile([P, D], U8, align_bytes=64)
-        nc.vector.quantize_mx(w1_q[:].bitcast(E4), w1_s[:], w1_bf[:])
+        for u in range(2):
+            interleave(nc.scalar.copy, w1_bf[:, u * PACK * (D // 2) : (u + 1) * PACK * (D // 2)], w1_raw[u][:])
+        w1_codes = keep.tile([P, D], U32, align_bytes=64)
+        w1_scales = keep.tile([P, D], U8, align_bytes=64)
+        nc.vector.quantize_mx(w1_codes[:].bitcast(E4M3), w1_scales[:], w1_bf[:])
 
         warm_sqrt = keep.tile([P, 1], F32)
-        nc.scalar.activation(warm_sqrt[:], w2_bf[:, 0:1], ACT.Sqrt, bias=one[:], scale=0.0)
-        ms = keep.tile([P, CH], F32)
-        rstd = keep.tile([P, CH], F32)
-        std = keep.tile([P, CH], F32)
-        r2 = keep.tile([P, CH], F32)
+        nc.scalar.activation(warm_sqrt[:], affine[:, PACK - 1, 0:1], ACT.Sqrt, bias=one[:], scale=0.0)
+
+        mean_square = keep.tile([P, CHUNKS], F32)
+        rstd = keep.tile([P, CHUNKS], F32)
+        std = keep.tile([P, CHUNKS], F32)
+        pull = keep.tile([P, CHUNKS], F32)
         xr_ps = []
 
         def norm(half):
             for c in (2 * half, 2 * half + 1):
-                ps = held.tile([P, PACK, P], F32, tag="held", name="xr_ps%d" % c)
+                bank = held.tile([P, D], F32, tag="held", name="xr_ps%d" % c)
                 for j in range(PACK):
-                    nc.tensor.transpose(ps[:, j, :], xr[j][:, c * P : (c + 1) * P], ident[:])
-                sq = ring.tile([P, D], BF16, tag="sq")
-                nc.scalar.activation(sq[:], ps[:].rearrange("i j p -> i (j p)"), ACT.Square, scale=D ** -0.5,
-                                     accum_out=ms[:, c : c + 1])
-                xr_ps.append(ps)
-            hc = slice(2 * half, 2 * half + 2)
-            nc.scalar.activation(std[:, hc], ms[:, hc], ACT.Sqrt)
-            nc.vector.reciprocal(rstd[:, hc], std[:, hc])
-            nc.vector.scalar_tensor_tensor(r2[:, hc], rstd[:, hc], -1.0 / D, rstd[:, hc], ALU.mult, ALU.mult)
+                    nc.tensor.transpose(bank[:, j * P : (j + 1) * P], xr[j][:, chunk_slots(c)], ident[:])
+                squares = ring.tile([P, D], BF16, tag="squares")
+                nc.scalar.activation(squares[:], bank[:], ACT.Square, scale=D ** -0.5,
+                                     accum_out=mean_square[:, c : c + 1])
+                xr_ps.append(bank)
+            two = slice(2 * half, 2 * half + 2)
+            nc.scalar.activation(std[:, two], mean_square[:, two], ACT.Sqrt)
+            nc.vector.reciprocal(rstd[:, two], std[:, two])
+            nc.vector.scalar_tensor_tensor(pull[:, two], rstd[:, two], -1.0 / D, rstd[:, two], ALU.mult, ALU.mult)
 
         norm(0)
-        da_q = keep.tile([P, N], U32, align_bytes=64)
-        da_s = keep.tile([P, N], U8, align_bytes=64)
-        da_words = []
-        das = []
-        for c in range(CH):
-            cols = slice(c * P, (c + 1) * P)
-            g_ps = g_banks[c]
+
+        da_codes = keep.tile([P, N], U32, align_bytes=64)
+        da_scales = keep.tile([P, N], U8, align_bytes=64)
+        da_by_slot = []
+        for c in range(CHUNKS):
             da = keep.tile([P, F], BF16, name="da%d" % c, align_bytes=64)
             nc.vector.tensor_tensor(
                 da[:].rearrange("i (u p e) -> i u p e", u=2, e=2),
-                g_ps[:].rearrange("i (u e) p -> i u p e", u=2),
-                dhg[c][:].rearrange("i (u p e) -> i u p e", u=2, e=2),
+                slope_ps[c][:].rearrange("i (u e) p -> i u p e", u=2),
+                dh_gated[c][:].rearrange("i (u p e) -> i u p e", u=2, e=2),
                 ALU.mult)
-            das.append(da)
-        for c in range(CH):
-            da = das[c]
-            w_ps = turn.tile([P, 2, P], F32, tag="turn")
+            da_by_slot.append(da)
+        da_by_f = []
+        for c in range(CHUNKS):
+            pairs_ps = turn.tile([P, 2, P], F32, tag="turn")
             for u in range(2):
-                nc.tensor.transpose(w_ps[:, u, :], da[:].bitcast(F32)[:, u * P : (u + 1) * P], ident[:])
-            da_t = keep.tile([P, F], BF16, name="da_t%d" % c, align_bytes=64)
-            nc.scalar.copy(da_t[:].bitcast(F32).rearrange("p (i u) -> p i u", u=2), w_ps[:].rearrange("p u i -> p i u"))
-            da_words.append(da_t)
+                nc.tensor.transpose(pairs_ps[:, u, :], da_by_slot[c][:].bitcast(F32)[:, u * P : (u + 1) * P], ident[:])
+            turned = keep.tile([P, F], BF16, name="da_turned%d" % c, align_bytes=64)
+            nc.scalar.copy(turned[:].bitcast(F32).rearrange("p (i u) -> p i u", u=2),
+                           pairs_ps[:].rearrange("p u i -> p i u"))
+            da_by_f.append(turned)
 
         norm(1)
 
-        hs = planes("h", F32, D)
-        mm = planes("m", F32, D)
-        cc = keep.tile([P, CH], F32)
-        for c in range(CH):
-            cols = slice(c * P, (c + 1) * P)
-            nc.vector.quantize_mx(da_q[:, cols].bitcast(E5), da_s[:, cols], da_words[c][:])
-        dx = planes("dx", F32, N)
+        direct = four_tiles("direct", D)
+        along = four_tiles("along", D)
+        along_factor = keep.tile([P, CHUNKS], F32)
+        for c in range(CHUNKS):
+            nc.vector.quantize_mx(da_codes[:, chunk_slots(c)].bitcast(E5M2), da_scales[:, chunk_slots(c)], da_by_f[c][:])
+        dx = four_tiles("dx", N)
+
+        def turn_back(planes, chunks):
+            bank = turn.tile([P, len(planes), len(chunks), P], F32, tag="turn")
+            parts = [(term, k, e) for term in (direct, along) for k in range(len(chunks)) for e in range(len(planes))]
+            for n, (term, k, e) in enumerate(parts):
+                nc.tensor.matmul(bank[:, e, k, :], term[chunks[k]][:, planes[e] * P : (planes[e] + 1) * P], ident[:],
+                                 start=(n == 0), stop=(n == len(parts) - 1), is_transpose=True)
+            for e, j in enumerate(planes):
+                nc.scalar.activation(dx[j][:, chunks[0] * P : (chunks[-1] + 1) * P],
+                                     bank[:, e, :, :].rearrange("p k i -> p (k i)"), ACT.Copy, scale=cd_col[:, j : j + 1])
+
         for half in range(2):
-            for c in (2 * half, 2 * half + 1):
-                cols = slice(c * P, (c + 1) * P)
+            chunks = (2 * half, 2 * half + 1)
+            for c in chunks:
                 dn_ps = turn.tile([P, D], F32, tag="turn")
-                nc.tensor.matmul_mx(dn_ps[:], lhsT=da_q[:, cols].bitcast(E5), lhsT_scale=da_s[:, cols],
-                                    rhs=w1_q[:].bitcast(E4), rhs_scale=w1_s[:], start=True, stop=True)
+                nc.tensor.matmul_mx(dn_ps[:], lhsT=da_codes[:, chunk_slots(c)].bitcast(E5M2),
+                                    lhsT_scale=da_scales[:, chunk_slots(c)],
+                                    rhs=w1_codes[:].bitcast(E4M3), rhs_scale=w1_scales[:], start=True, stop=True)
                 nc.vector.scalar_tensor_tensor(
-                    hs[c][:].rearrange("i (j p) -> i j p", j=PACK),
+                    direct[c][:].rearrange("i (j p) -> i j p", j=PACK),
                     dn_ps[:].rearrange("i (p j) -> i j p", j=PACK),
                     rstd[:, c : c + 1], gam_row[:], ALU.mult, ALU.mult)
-            for c in (2 * half, 2 * half + 1):
-                xr_flat = xr_ps[c][:].rearrange("i j p -> i (j p)")
-                prod = ring.tile([P, D], F32, tag="prod")
-                nc.vector.scalar_tensor_tensor(prod[:], xr_flat, r2[:, c : c + 1], hs[c][:], ALU.mult, ALU.mult,
-                                               accum_out=cc[:, c : c + 1])
-                nc.scalar.activation(mm[c][:], xr_flat, ACT.Copy, scale=cc[:, c : c + 1])
-
-            for pair in range(2):
-                f_ps = turn.tile([P, 2, HALF], F32, tag="turn")
-                parts = [(src, k, e) for src in (hs, mm) for k in range(2) for e in range(2)]
-                for n, (src, k, e) in enumerate(parts):
-                    j = 2 * pair + e
-                    nc.tensor.matmul(f_ps[:, e, k * P : (k + 1) * P], src[2 * half + k][:, j * P : (j + 1) * P], ident[:],
-                                     start=(n == 0), stop=(n == len(parts) - 1), is_transpose=True)
-                for e in range(2):
-                    j = 2 * pair + e
-                    nc.scalar.activation(dx[j][:, half * HALF : (half + 1) * HALF], f_ps[:, e, :], ACT.Copy,
-                                         scale=cd_col[:, j : j + 1])
+            for c in chunks:
+                products = ring.tile([P, D], F32, tag="products")
+                nc.vector.scalar_tensor_tensor(products[:], xr_ps[c][:], pull[:, c : c + 1], direct[c][:],
+                                               ALU.mult, ALU.mult, accum_out=along_factor[:, c : c + 1])
+                nc.scalar.activation(along[c][:], xr_ps[c][:], ACT.Copy, scale=along_factor[:, c : c + 1])
+            turn_back((0, 1), chunks)
+        for j in (2, 3):
+            turn_back((j,), tuple(range(CHUNKS)))
 
         def scatter(j, lo, hi):
-            nc.vector.tensor_tensor(out_win[j][:].indirect(offsets[:, lo // 16 : hi // 16]),
-                                    dx[j][:, lo:hi], dy[:, j, lo:hi], ALU.add)
+            nc.vector.tensor_tensor(listed(out_win[j], lo, hi), dx[j][:, lo:hi], dy[:, j, lo:hi], ALU.add)
 
         out_bf = keep.tile([P, T, PACK], BF16, align_bytes=64)
-        split = T // 2
+        last_parts = ((0, SCALAR_TOKENS // 2), (SCALAR_TOKENS // 2, SCALAR_TOKENS))
+        scalar_parts = (((0, T),), ((0, T),), ((0, SCALAR_TOKENS),), last_parts)
         scatter(0, 0, HALF)
         scatter(1, 0, HALF)
         for j in range(PACK):
-            if j < 2:
-                scatter(j, HALF, N)
-            else:
-                scatter(j, 0, N)
-            nc.sync.dma_start(rows(out_0)[:, j, :], out_win[j][:])
-            upto = T if j < 2 else split
-            for lo, hi in ((0, upto),) if j < PACK - 1 else ((0, upto // 2), (upto // 2, upto)):
+            scatter(j, HALF if j < 2 else 0, N)
+            nc.sync.dma_start(by_planes(out_0)[:, j, :], out_win[j][:])
+            for lo, hi in scalar_parts[j]:
                 nc.scalar.copy(out_bf[:, lo:hi, j], out_win[j][:, lo:hi])
-        for j in range(2, PACK):
-            nc.vector.tensor_copy(out_bf[:, split:T, j], out_win[j][:, split:T])
+        for j in (2, 3):
+            nc.vector.tensor_copy(out_bf[:, SCALAR_TOKENS:T, j], out_win[j][:, SCALAR_TOKENS:T])
 
-        out_q = keep.tile([P, T], U32, align_bytes=64)
-        out_s = keep.tile([P, T], U8, align_bytes=64)
+        out_codes = keep.tile([P, T], U32, align_bytes=64)
+        out_scales = keep.tile([P, T], U8, align_bytes=64)
         words = out_1.rearrange("a p c l -> p (a c l)").bitcast(I32)
-        for lo, hi in ((split, T), (0, split // 2), (split // 2, split)):
-            cols = slice(lo, hi)
-            nc.vector.quantize_mx(out_q[:, cols].bitcast(E4), out_s[:, cols],
-                                  out_bf[:, cols, :].rearrange("p c l -> p (c l)"))
-            nc.sync.dma_start(words[:, cols], out_q[:, cols].bitcast(I32))
-        scales = out_2.rearrange("a f c -> (a f) c").bitcast(I32)
+        for lo, hi in ((SCALAR_TOKENS, T),) + last_parts:
+            nc.vector.quantize_mx(out_codes[:, lo:hi].bitcast(E4M3), out_scales[:, lo:hi],
+                                  out_bf[:, lo:hi, :].rearrange("p c l -> p (c l)"))
+            nc.sync.dma_start(words[:, lo:hi], out_codes[:, lo:hi].bitcast(I32))
+        scale_rows = out_2.rearrange("a f c -> (a f) c").bitcast(I32)
         for q in range(4):
             queue = nc.sync if q % 2 else nc.scalar
-            queue.dma_start(scales[4 * q : 4 * q + 4, :], out_s[32 * q : 32 * q + 4, :].bitcast(I32))
+            queue.dma_start(scale_rows[4 * q : 4 * q + 4, :], out_scales[32 * q : 32 * q + 4, :].bitcast(I32))

from contextlib import ExitStack

import concourse.mybir as mybir
from concourse.masks import make_identity

P = 128
PACK = 4
D = 512
F = 512
T = 1024
N = 512
CHUNKS = N // P
HALF = N // 2
LIST_ROWS = 16
GPSIMD_AFFINES = 2
SCALAR_TOKENS = T // 2

FLOPS = 2 * 2 * D * F * N

F32 = mybir.dt.float32
BF16 = mybir.dt.bfloat16
U32 = mybir.dt.uint32
I32 = mybir.dt.int32
U16 = mybir.dt.uint16
U8 = mybir.dt.uint8
E4M3 = mybir.dt.float8_e4m3fn_x4
E5M2 = mybir.dt.float8_e5m2_x4
ALU = mybir.AluOpType
ACT = mybir.ActivationFunctionType


def tile_attend_gblock_sil_pl_kernel(tc, xT, dyT, aT, w1, w2, gt, gam, cf, cd, offs, out_0, out_1, out_2):
    nc = tc.nc
    with ExitStack() as ctx:
        keep = ctx.enter_context(tc.tile_pool(name="keep", bufs=1))
        ring = ctx.enter_context(tc.tile_pool(name="ring", bufs=2))
        held = ctx.enter_context(tc.psum_pool(name="held", bufs=CHUNKS))
        turn = ctx.enter_context(tc.psum_pool(name="turn", bufs=CHUNKS))

        def four_tiles(name, width):
            return [keep.tile([P, width], F32, name="%s%d" % (name, j), align_bytes=64) for j in range(PACK)]

        def by_planes(table):
            return table.rearrange("(p j) t -> p j t", j=PACK)

        def interleave(engine_copy, dst, src):
            engine_copy(
                dst.rearrange("p (c i t) -> p c t i", i=4, t=PACK),
                src.rearrange("p t (c i) -> p c t i", i=4),
            )

        def chunk_slots(c):
            return slice(c * P, (c + 1) * P)

        def listed(window, lo=0, hi=N):
            return window[:].indirect(offsets[:, lo // LIST_ROWS : hi // LIST_ROWS])

        offsets = keep.tile([P, N // LIST_ROWS], U16, name="offsets")
        nc.sync.dma_start(offsets[:], offs)
        dy_win, a_win = four_tiles("dy_win", T), four_tiles("a_win", T)
        x_win, out_win = four_tiles("x_win", T), four_tiles("out_win", T)
        cd_col = keep.tile([P, PACK], F32)
        gam_col = keep.tile([P, PACK], F32)
        cf_col = keep.tile([P, PACK], F32)
        one = keep.tile([P, 1], F32)
        nc.gpsimd.memset(one[:], 1.0)
        ident = keep.tile([P, P], F32)
        make_identity(nc, ident[:])
        gt_win = keep.tile([P, T], F32)
        nc.vector.memset(gt_win[:], 0.0)

        w2_raw = keep.tile([P, PACK, F], F32)
        w1_raw = [keep.tile([P, PACK, D // 2], F32, name="w1_raw%d" % u) for u in range(2)]
        nc.sync.dma_start(cd_col[:], cd[0:1, :].rearrange("o (p j) -> (o p) j", j=PACK))
        nc.sync.dma_start(cf_col[:], cf.rearrange("(p j) o -> p (j o)", j=PACK))
        for j in range(PACK):
            nc.sync.dma_start(a_win[j][:], by_planes(aT)[:, j, :])
        nc.sync.dma_start(gam_col[:], gam[0:1, :].rearrange("o (p j) -> (o p) j", j=PACK))
        nc.sync.dma_start(gt_win[0:1, :], gt[0:1, :])
        for j in range(PACK):
            nc.sync.dma_start(dy_win[j][:], by_planes(dyT)[:, j, :])
        nc.sync.dma_start(w2_raw[:], by_planes(w2))
        for j in range(PACK):
            nc.sync.dma_start(x_win[j][:], by_planes(xT)[:, j, :])
        for u in range(2):
            nc.sync.dma_start(w1_raw[u][:], by_planes(w1)[:, :, u * (D // 2) : (u + 1) * (D // 2)])
        for j in range(PACK):
            nc.sync.dma_start(out_win[j][:], by_planes(dyT)[:, j, :])

        warm_silu = keep.tile([P, 1], F32)
        nc.scalar.activation(warm_silu[:], one[:], ACT.Silu)

        cf_half = keep.tile([P, PACK], F32)
        cf_minus_half = keep.tile([P, PACK], F32)
        nc.gpsimd.tensor_scalar(cf_half[:], cf_col[:], 0.5, 0.0, ALU.mult, ALU.add)
        nc.gpsimd.tensor_scalar(cf_minus_half[:], cf_col[:], -0.5, 0.0, ALU.mult, ALU.add)
        cd_wide = four_tiles("cd_wide", N)
        for j in range(PACK):
            nc.scalar.copy(cd_wide[j][:], cd_col[:, j : j + 1].to_broadcast([P, N]))
        gam_ps = held.tile([P, PACK, P], F32, tag="held")
        for j in range(PACK):
            nc.tensor.transpose(gam_ps[:, j, :], gam_col[:, j : j + 1].to_broadcast([P, P]), ident[:])
        gam_row = keep.tile([P, PACK, P], F32)
        nc.scalar.copy(gam_row[:], gam_ps[:])

        tanh = keep.tile([P, PACK, N], F32)
        affine = keep.tile([P, PACK, N], F32)
        cross = keep.tile([P, PACK, N], F32)
        for j in range(PACK):
            a = keep.tile([P, N], F32, name="a%d" % j)
            nc.vector.tensor_copy(a[:], listed(a_win[j]))
            silu = ring.tile([P, N], F32, tag="silu", bufs=3)
            nc.scalar.activation(silu[:], a[:], ACT.Silu)
            nc.scalar.activation(tanh[:, j, :], a[:], ACT.Tanh, scale=-0.5)
            factor, shift = cf_half[:, j : j + 1], cf_minus_half[:, j : j + 1]
            if j < GPSIMD_AFFINES:
                nc.gpsimd.tensor_scalar(affine[:, j, :], silu[:], factor, shift, ALU.mult, ALU.add)
            else:
                nc.scalar.activation(affine[:, j, :], silu[:], ACT.Identity, bias=shift, scale=factor)
            nc.gpsimd.tensor_tensor(cross[:, j, :], affine[:, j, :], tanh[:, j, :], ALU.mult)

        gt_row = keep.tile([P, N], F32)
        nc.vector.tensor_copy(gt_row[:], listed(gt_win))
        gt_ps = held.tile([P, CHUNKS, P], F32, tag="held")
        for c in range(CHUNKS):
            nc.tensor.transpose(gt_ps[:, c, :], gt_row[:, chunk_slots(c)], ident[:])
        gt_col = keep.tile([P, CHUNKS], F32)
        nc.scalar.copy(gt_col[:], gt_ps[:, :, 0])

        w2_bf = keep.tile([P, PACK * F], BF16, align_bytes=64)
        interleave(nc.vector.tensor_copy, w2_bf[:], w2_raw[:])
        w2_codes = keep.tile([P, F], U32, align_bytes=64)
        w2_scales = keep.tile([P, F], U8, align_bytes=64)
        nc.vector.quantize_mx(w2_codes[:].bitcast(E4M3), w2_scales[:], w2_bf[:])

        dy = keep.tile([P, PACK, N], F32)
        for j in range(PACK):
            nc.vector.tensor_copy(dy[:, j, :], listed(dy_win[j]))
        dy_bf = keep.tile([P, PACK * N], BF16, align_bytes=64)
        interleave(nc.scalar.copy, dy_bf[:], dy[:])
        dy_codes = keep.tile([P, N], U32, align_bytes=64)
        dy_scales = keep.tile([P, N], U8, align_bytes=64)
        nc.vector.quantize_mx(dy_codes[:].bitcast(E5M2), dy_scales[:], dy_bf[:])

        slope_ps = []
        for c in range(CHUNKS):
            bank = turn.tile([P, PACK, P], F32, tag="turn")
            for j in range(PACK):
                nc.tensor.matmul(bank[:, j, :], cf_col[:, j : j + 1].to_broadcast([P, P]), ident[:],
                                 start=(j == 0), stop=False, is_transpose=True)
            for j in range(PACK):
                nc.tensor.matmul(bank[:, j, :], affine[:, j, chunk_slots(c)], ident[:],
                                 start=False, stop=False, is_transpose=True)
            for j in range(PACK):
                nc.tensor.matmul(bank[:, j, :], cross[:, j, chunk_slots(c)], ident[:],
                                 start=False, stop=(j == PACK - 1), is_transpose=True)
            slope_ps.append(bank)

        dh_gated = four_tiles("dh_gated", F)
        for c in range(CHUNKS):
            dh_ps = held.tile([P, F], F32, tag="held")
            nc.tensor.matmul_mx(dh_ps[:], lhsT=dy_codes[:, chunk_slots(c)].bitcast(E5M2),
                                lhsT_scale=dy_scales[:, chunk_slots(c)],
                                rhs=w2_codes[:].bitcast(E4M3), rhs_scale=w2_scales[:], start=True, stop=True)
            nc.scalar.activation(
                dh_gated[c][:].rearrange("i (u p e) -> i u p e", u=2, e=2),
                dh_ps[:].rearrange("i (p u e) -> i u p e", u=2, e=2),
                ACT.Copy, scale=gt_col[:, c : c + 1])

        xr = four_tiles("xr", N)
        for j in range(PACK):
            nc.vector.tensor_tensor(xr[j][:], listed(x_win[j]), cd_wide[j][:], ALU.mult)

        w1_bf = keep.tile([P, PACK * D], BF16, align_bytes=64)
        for u in range(2):
            interleave(nc.scalar.copy, w1_bf[:, u * PACK * (D // 2) : (u + 1) * PACK * (D // 2)], w1_raw[u][:])
        w1_codes = keep.tile([P, D], U32, align_bytes=64)
        w1_scales = keep.tile([P, D], U8, align_bytes=64)
        nc.vector.quantize_mx(w1_codes[:].bitcast(E4M3), w1_scales[:], w1_bf[:])

        warm_sqrt = keep.tile([P, 1], F32)
        nc.scalar.activation(warm_sqrt[:], affine[:, PACK - 1, 0:1], ACT.Sqrt, bias=one[:], scale=0.0)

        mean_square = keep.tile([P, CHUNKS], F32)
        rstd = keep.tile([P, CHUNKS], F32)
        std = keep.tile([P, CHUNKS], F32)
        pull = keep.tile([P, CHUNKS], F32)
        xr_ps = []

        def norm(half):
            for c in (2 * half, 2 * half + 1):
                bank = held.tile([P, D], F32, tag="held", name="xr_ps%d" % c)
                for j in range(PACK):
                    nc.tensor.transpose(bank[:, j * P : (j + 1) * P], xr[j][:, chunk_slots(c)], ident[:])
                squares = ring.tile([P, D], BF16, tag="squares")
                nc.scalar.activation(squares[:], bank[:], ACT.Square, scale=D ** -0.5,
                                     accum_out=mean_square[:, c : c + 1])
                xr_ps.append(bank)
            two = slice(2 * half, 2 * half + 2)
            nc.scalar.activation(std[:, two], mean_square[:, two], ACT.Sqrt)
            nc.vector.reciprocal(rstd[:, two], std[:, two])
            nc.vector.scalar_tensor_tensor(pull[:, two], rstd[:, two], -1.0 / D, rstd[:, two], ALU.mult, ALU.mult)

        norm(0)

        da_codes = keep.tile([P, N], U32, align_bytes=64)
        da_scales = keep.tile([P, N], U8, align_bytes=64)
        da_by_slot = []
        for c in range(CHUNKS):
            da = keep.tile([P, F], BF16, name="da%d" % c, align_bytes=64)
            nc.vector.tensor_tensor(
                da[:].rearrange("i (u p e) -> i u p e", u=2, e=2),
                slope_ps[c][:].rearrange("i (u e) p -> i u p e", u=2),
                dh_gated[c][:].rearrange("i (u p e) -> i u p e", u=2, e=2),
                ALU.mult)
            da_by_slot.append(da)
        da_by_f = []
        for c in range(CHUNKS):
            pairs_ps = turn.tile([P, 2, P], F32, tag="turn")
            for u in range(2):
                nc.tensor.transpose(pairs_ps[:, u, :], da_by_slot[c][:].bitcast(F32)[:, u * P : (u + 1) * P], ident[:])
            turned = keep.tile([P, F], BF16, name="da_turned%d" % c, align_bytes=64)
            nc.scalar.copy(turned[:].bitcast(F32).rearrange("p (i u) -> p i u", u=2),
                           pairs_ps[:].rearrange("p u i -> p i u"))
            da_by_f.append(turned)

        norm(1)

        direct = four_tiles("direct", D)
        along = four_tiles("along", D)
        along_factor = keep.tile([P, CHUNKS], F32)
        for c in range(CHUNKS):
            nc.vector.quantize_mx(da_codes[:, chunk_slots(c)].bitcast(E5M2), da_scales[:, chunk_slots(c)], da_by_f[c][:])
        dx = four_tiles("dx", N)

        def turn_back(planes, chunks):
            bank = turn.tile([P, len(planes), len(chunks), P], F32, tag="turn")
            parts = [(term, k, e) for term in (direct, along) for k in range(len(chunks)) for e in range(len(planes))]
            for n, (term, k, e) in enumerate(parts):
                nc.tensor.matmul(bank[:, e, k, :], term[chunks[k]][:, planes[e] * P : (planes[e] + 1) * P], ident[:],
                                 start=(n == 0), stop=(n == len(parts) - 1), is_transpose=True)
            for e, j in enumerate(planes):
                nc.scalar.activation(dx[j][:, chunks[0] * P : (chunks[-1] + 1) * P],
                                     bank[:, e, :, :].rearrange("p k i -> p (k i)"), ACT.Copy, scale=cd_col[:, j : j + 1])

        for half in range(2):
            chunks = (2 * half, 2 * half + 1)
            for c in chunks:
                dn_ps = turn.tile([P, D], F32, tag="turn")
                nc.tensor.matmul_mx(dn_ps[:], lhsT=da_codes[:, chunk_slots(c)].bitcast(E5M2),
                                    lhsT_scale=da_scales[:, chunk_slots(c)],
                                    rhs=w1_codes[:].bitcast(E4M3), rhs_scale=w1_scales[:], start=True, stop=True)
                nc.vector.scalar_tensor_tensor(
                    direct[c][:].rearrange("i (j p) -> i j p", j=PACK),
                    dn_ps[:].rearrange("i (p j) -> i j p", j=PACK),
                    rstd[:, c : c + 1], gam_row[:], ALU.mult, ALU.mult)
            for c in chunks:
                products = ring.tile([P, D], F32, tag="products")
                nc.vector.scalar_tensor_tensor(products[:], xr_ps[c][:], pull[:, c : c + 1], direct[c][:],
                                               ALU.mult, ALU.mult, accum_out=along_factor[:, c : c + 1])
                nc.scalar.activation(along[c][:], xr_ps[c][:], ACT.Copy, scale=along_factor[:, c : c + 1])
            turn_back((0, 1), chunks)
        for j in (2, 3):
            turn_back((j,), tuple(range(CHUNKS)))

        def scatter(j, lo, hi):
            nc.vector.tensor_tensor(listed(out_win[j], lo, hi), dx[j][:, lo:hi], dy[:, j, lo:hi], ALU.add)

        out_bf = keep.tile([P, T, PACK], BF16, align_bytes=64)
        last_parts = ((0, SCALAR_TOKENS // 2), (SCALAR_TOKENS // 2, SCALAR_TOKENS))
        scalar_parts = (((0, T),), ((0, T),), ((0, SCALAR_TOKENS),), last_parts)
        scatter(0, 0, HALF)
        scatter(1, 0, HALF)
        for j in range(PACK):
            scatter(j, HALF if j < 2 else 0, N)
            nc.sync.dma_start(by_planes(out_0)[:, j, :], out_win[j][:])
            for lo, hi in scalar_parts[j]:
                nc.scalar.copy(out_bf[:, lo:hi, j], out_win[j][:, lo:hi])
        for j in (2, 3):
            nc.vector.tensor_copy(out_bf[:, SCALAR_TOKENS:T, j], out_win[j][:, SCALAR_TOKENS:T])

        out_codes = keep.tile([P, T], U32, align_bytes=64)
        out_scales = keep.tile([P, T], U8, align_bytes=64)
        words = out_1.rearrange("a p c l -> p (a c l)").bitcast(I32)
        for lo, hi in ((SCALAR_TOKENS, T),) + last_parts:
            nc.vector.quantize_mx(out_codes[:, lo:hi].bitcast(E4M3), out_scales[:, lo:hi],
                                  out_bf[:, lo:hi, :].rearrange("p c l -> p (c l)"))
            nc.sync.dma_start(words[:, lo:hi], out_codes[:, lo:hi].bitcast(I32))
        scale_rows = out_2.rearrange("a f c -> (a f) c").bitcast(I32)
        for q in range(4):
            queue = nc.sync if q % 2 else nc.scalar
            queue.dma_start(scale_rows[4 * q : 4 * q + 4, :], out_scales[32 * q : 32 * q + 4, :].bitcast(I32))
